import numpy as np
import ml_dtypes


def mxq(x, axis, fmt="e4m3"):
    dtype, down = {"e4m3": (ml_dtypes.float8_e4m3fn, 7), "e5m2": (ml_dtypes.float8_e5m2, 14)}[fmt]
    v = np.moveaxis(np.asarray(x, np.float32).astype(ml_dtypes.bfloat16).astype(np.float64), axis, -1)
    blocks = v.reshape(v.shape[:-1] + (-1, 32))
    amax = np.abs(blocks).max(-1, keepdims=True)
    byte = np.maximum(np.where(amax > 0, np.frexp(amax)[1] - 1 + 127, 0) - down, 1)
    scale = np.exp2(byte - 127.0)
    codes = (blocks / scale).astype(np.float32).astype(dtype).astype(np.float64)
    return np.moveaxis((codes * scale).reshape(v.shape), -1, axis)


WIDE = False


def mx_kscale(k):
    if not WIDE:
        return np.ones(k)
    levels = np.array([10, -10, 5, -5, 0])
    if k % 512:
        return np.exp2(np.random.permutation(np.resize(levels, k // 32))).repeat(32)
    a = np.empty((k // 512, 16))
    for p in range(k // 512):
        a[p, :8] = np.random.permutation(np.resize(levels, 8))
        for g in range(8):
            far = levels[np.abs(levels - a[p, g]) >= 10]
            a[p, g + 8] = far[np.random.randint(len(far))]
    return np.exp2(a.ravel()).repeat(32)


def f64(x):
    return np.asarray(x).astype(np.float64)


def striped(idx):
    return np.tile(idx.reshape(-1, 16).T, (8, 1)).astype(np.uint16)


def unstriped(offs):
    return offs[:16].T.reshape(-1).astype(np.int64)


def silu(v):
    return v / (1.0 + np.exp(-np.maximum(v, -700.0)))


K, T, E, C, H, N = 512, 512, 8, 128, 512, 512


def by_expert(wq, xq):
    return np.concatenate([wq[e].T @ xq[:, e * C:(e + 1) * C] for e in range(E)], axis=1)


def setup_inputs():
    n = np.random.standard_normal
    s = mx_kscale(K)[:, None]
    u = mx_kscale(H)
    first = np.random.permutation(np.repeat(np.arange(E), T // E))
    second = (first + 1 + np.random.permutation(np.repeat(np.arange(E - 1), -(-T // (E - 1)))[:T])) % E
    while np.bincount(second, minlength=E).max() != T // E:
        load = np.bincount(second, minlength=E); hi, lo = int(load.argmax()), int(load.argmin())
        t = np.flatnonzero((second == hi) & (first != lo))[0]; second[t] = lo
    slot_token = np.empty(E * C, np.int64); pos = np.empty((2, T), np.int64); fill = np.zeros(E, np.int64)
    place = np.stack([np.random.permutation(C) for _ in range(E)])
    for r, deal in enumerate((first, second)):
        for t in np.random.permutation(T):
            e = deal[t]; j = e * C + place[e, fill[e]]; fill[e] += 1; slot_token[j] = t; pos[r, t] = j
    g = np.random.uniform(0.2, 0.8, T)
    return {
        "xT": (n((K, T)) * s).astype(np.float32),
        "w1": (n((E, K, H)) / np.sqrt(K) / s[None]).astype(np.float32),
        "w3": (n((E, K, H)) / np.sqrt(K) / s[None] * u[None, None, :]).astype(np.float32),
        "w2": (n((E, H, N)) / np.sqrt(H) / u[None, :, None]).astype(np.float32),
        "gate": np.stack([np.tile(g, (N, 1)), np.tile(1.0 - g, (N, 1))]).astype(np.float32),
        "offs": striped(slot_token),
        "pos1": striped(pos[0]),
        "pos2": striped(pos[1]),
    }


def reference(xT, w1, w3, w2, gate, offs, pos1, pos2):
    idx = unstriped(offs)
    xq = mxq(f64(xT)[:, idx], 0, "e4m3")
    h = silu(by_expert(mxq(f64(w1), 1, "e4m3"), xq))
    h = h * by_expert(mxq(f64(w3), 1, "e4m3"), xq)
    y = by_expert(mxq(f64(w2), 1, "e4m3"), mxq(h, 0, "e4m3"))
    return f64(gate[0]) * y[:, unstriped(pos1)] + f64(gate[1]) * y[:, unstriped(pos2)]

@@ -1,0 +1,236 @@
+from contextlib import ExitStack
+
+import concourse.mybir as mybir
+
+K, T, E, C, H, N = 512, 512, 8, 128, 512, 512
+P = 128
+FLOPS = 2 * E * C * (2 * K * H + H * N)
+
+F32 = mybir.dt.float32
+BF16 = mybir.dt.bfloat16
+U32 = mybir.dt.uint32
+U16 = mybir.dt.uint16
+U8 = mybir.dt.uint8
+FP8X4 = mybir.dt.float8_e4m3fn_x4
+MULT = mybir.AluOpType.mult
+ADD = mybir.AluOpType.add
+SILU = mybir.ActivationFunctionType.Silu
+
+WHOLE = 2
+RAW_BUFS = 10
+PRE = 9
+S_SHARE = 80
+S_SHARE_X = 44
+S_SHARE_QA = 128
+S_SHARE_QB = 64
+
+
+def tile_routed_moe_kernel(tc, xT, w1, w3, w2, gate, offs, pos1, pos2, out):
+    nc = tc.nc
+    with ExitStack() as ctx:
+        lists = ctx.enter_context(tc.tile_pool(name="lists", bufs=1))
+        keep = ctx.enter_context(tc.tile_pool(name="keep", bufs=1))
+        rawp = ctx.enter_context(tc.tile_pool(name="rawp", bufs=RAW_BUFS))
+        grpp = ctx.enter_context(tc.tile_pool(name="grpp", bufs=4))
+        codp = ctx.enter_context(tc.tile_pool(name="codp", bufs=4))
+        work = ctx.enter_context(tc.tile_pool(name="work", bufs=2))
+        psab = ctx.enter_context(tc.psum_pool(name="psab", bufs=2))
+        psy = ctx.enter_context(tc.psum_pool(name="psy", bufs=2))
+
+        offs_t = lists.tile([P, E * C // 16], U16, name="offs_t")
+        nc.sync.dma_start(offs_t[:], offs)
+        pos1_t = lists.tile([P, T // 16], U16, name="pos1_t")
+        nc.sync.dma_start(pos1_t[:], pos1)
+        pos2_t = lists.tile([P, T // 16], U16, name="pos2_t")
+        nc.sync.dma_start(pos2_t[:], pos2)
+        pos_t = [pos1_t, pos2_t]
+
+        warm = keep.tile([P, 1], F32, name="warm")
+        nc.vector.memset(warm[:], 0.0)
+        warm2 = keep.tile([P, 1], F32, name="warm2")
+        nc.scalar.activation(out=warm2[:], in_=warm[:], func=SILU)
+
+        x_words = keep.tile([P, T], U32, name="x_words", align_bytes=64)
+        x_bytes = keep.tile([P, T], U8, name="x_bytes", align_bytes=64)
+        nc.gpsimd.memset(x_bytes[:], 0)
+        g_words = [keep.tile([P, 2 * C], U32, name="g_words%d" % s, align_bytes=64) for s in range(4)]
+        g_bytes = [keep.tile([P, 2 * C], U8, name="g_bytes%d" % s, align_bytes=64) for s in range(4)]
+        h_words = [keep.tile([P, C], U32, name="h_words%d" % e, align_bytes=64) for e in range(E)]
+        h_bytes = [keep.tile([P, C], U8, name="h_bytes%d" % e, align_bytes=64) for e in range(E)]
+        ywin = [keep.tile([P, E * C], F32, name="ywin%d" % b) for b in range(4)]
+        gates = [None] * 4
+
+        jobs = [{"kind": "x", "width": 512}]
+        for e in range(E):
+            jobs.append({"kind": "w1", "e": e, "width": 512})
+            jobs.append({"kind": "w3", "e": e, "width": 512})
+            if 1 <= e <= WHOLE:
+                jobs.append({"kind": "w2", "e": e - 1, "width": 512})
+        for b in range(4):
+            jobs.append({"kind": "q", "b": b, "experts": [2, 3, 4, 5], "width": 512, "share": 32 if b == 0 else S_SHARE_QA})
+            jobs.append({"kind": "q", "b": b, "experts": [6, 7], "width": 256, "share": 16 if b == 0 else S_SHARE_QB})
+            jobs.append({"kind": "g", "b": b})
+
+        state = {"ya": [None, None], "w1": {}, "later": []}
+
+        def load(job):
+            kind = job["kind"]
+            if kind == "g":
+                b = job["b"]
+                gates[b] = rawp.tile([P, 2, T], F32, name="raw", tag="raw")
+                nc.sync.dma_start(out=gates[b][:], in_=gate[:, b * P:(b + 1) * P, :].rearrange("r p t -> p r t"))
+                return
+            raw = rawp.tile([P, 4, job["width"]], F32, name="raw", tag="raw")
+            job["raw"] = raw
+            if kind == "x":
+                nc.sync.dma_start(out=raw[:], in_=xT.rearrange("(p j) c -> p j c", j=4))
+            elif kind == "q":
+                b = job["b"]
+                for i, e in enumerate(job["experts"]):
+                    nc.sync.dma_start(
+                        out=raw[:, :, i * P:(i + 1) * P],
+                        in_=w2[e].rearrange("(p j) c -> p j c", j=4)[:, :, b * P:(b + 1) * P],
+                    )
+            else:
+                src = {"w1": w1, "w3": w3, "w2": w2}[kind]
+                nc.sync.dma_start(out=raw[:], in_=src[job["e"]].rearrange("(p j) c -> p j c", j=4))
+
+        def interleave(job):
+            kind = job["kind"]
+            if kind == "g":
+                return
+            raw = job["raw"]
+            groups = job["width"] // 4
+            share = job.get("share", S_SHARE_X if kind == "x" else S_SHARE)
+            if kind in ("w1", "w3"):
+                grp = grpp.tile([P, 4, 128, 4], BF16, name="grp", tag="grp", align_bytes=64)
+                job["flat"] = grp[:].rearrange("p t m j -> p (t m j)")
+            else:
+                grp = grpp.tile([P, job["width"], 4], BF16, name="grp", tag="grp", align_bytes=64)
+                job["flat"] = grp[:].rearrange("p c j -> p (c j)")
+            for eng, lo, hi in ((nc.scalar.copy, 0, share), (nc.vector.tensor_copy, share, groups)):
+                if lo == hi:
+                    continue
+                if kind in ("w1", "w3"):
+                    dst = grp[:, :, lo:hi, :].rearrange("p t m j -> p m j t")
+                    src = raw[:, :, 4 * lo:4 * hi].rearrange("p j (m t) -> p m j t", t=4)
+                else:
+                    dst = grp[:, 4 * lo:4 * hi, :].rearrange("p (c i) j -> p c j i", i=4)
+                    src = raw[:, :, 4 * lo:4 * hi].rearrange("p j (c i) -> p c j i", i=4)
+                eng(out=dst, in_=src)
+
+        def quantise(job):
+            kind = job["kind"]
+            if kind == "g":
+                return
+            if kind == "x":
+                words, scales = x_words, x_bytes
+            else:
+                words = codp.tile([P, job["width"]], U32, name="words", tag="words", align_bytes=64)
+                scales = codp.tile([P, job["width"]], U8, name="scales", tag="scales", align_bytes=64)
+            job["words"] = words
+            job["scales"] = scales
+            nc.vector.quantize_mx(out=words[:].bitcast(FP8X4), scales=scales[:], in_=job["flat"])
+
+        def gather_tokens(s):
+            sl = offs_t[:, s * 16:(s + 1) * 16]
+            nc.vector.tensor_copy(g_words[s][:], x_words[:].indirect(sl))
+            nc.vector.tensor_copy(g_bytes[s][:], x_bytes[:].indirect(sl))
+
+        def mx(out_ap, wjob, col, rhs_w, rhs_s):
+            cols = slice(col * P, (col + 1) * P)
+            nc.tensor.matmul_mx(
+                out=out_ap,
+                lhsT=wjob["words"][:, cols].bitcast(FP8X4),
+                lhsT_scale=wjob["scales"][:, cols],
+                rhs=rhs_w.bitcast(FP8X4),
+                rhs_scale=rhs_s,
+                start=True,
+                stop=True,
+            )
+
+        def quantise_h(e, hg):
+            nc.vector.quantize_mx(
+                out=h_words[e][:].bitcast(FP8X4), scales=h_bytes[e][:], in_=hg[:].rearrange("p n t -> p (n t)")
+            )
+
+        def combine(b):
+            parts = []
+            for r in range(2):
+                part = work.tile([P, T], F32, name="part%d" % r, tag="part%d" % r)
+                nc.vector.tensor_tensor(out=part[:], in0=ywin[b][:].indirect(pos_t[r][:]), in1=gates[b][:, r, :], op=MULT)
+                parts.append(part)
+            res = work.tile([P, T], F32, name="res", tag="res")
+            nc.vector.tensor_tensor(out=res[:], in0=parts[0][:], in1=parts[1][:], op=ADD)
+            nc.sync.dma_start(out=out[b * P:(b + 1) * P, :], in_=res[:])
+
+        def run_later():
+            later = state["later"]
+            state["later"] = []
+            for fn in later:
+                fn()
+
+        def compute(job):
+            kind = job["kind"]
+            run_later()
+            if kind == "x":
+                gather_tokens(0)
+            elif kind == "w1":
+                e = job["e"]
+                state["w1"][e] = job
+                if e % 2 == 1 and e < E - 1:
+                    gather_tokens((e + 1) // 2)
+            elif kind == "w3":
+                e = job["e"]
+                xw = g_words[e // 2][:, (e % 2) * C:(e % 2 + 1) * C]
+                xs = g_bytes[e // 2][:, (e % 2) * C:(e % 2 + 1) * C]
+                pa = psab.tile([P, 4, C], F32, name="pa", tag="pa")
+                pb = psab.tile([P, 4, C], F32, name="pb", tag="pb")
+                for t in range(4):
+                    mx(pa[:, t, :], state["w1"][e], t, xw, xs)
+                for t in range(4):
+                    mx(pb[:, t, :], job, t, xw, xs)
+                sil = work.tile([P, C, 4], F32, name="sil", tag="sil")
+                nc.scalar.activation(out=sil[:], in_=pa[:].rearrange("p t n -> p n t"), func=SILU)
+                hg = work.tile([P, C, 4], BF16, name="hg", tag="hg", align_bytes=64)
+                nc.vector.tensor_tensor(out=hg[:], in0=pb[:].rearrange("p t n -> p n t"), in1=sil[:], op=MULT)
+                state["later"].append(lambda: quantise_h(e, hg))
+            elif kind == "w2":
+                e = job["e"]
+                if e == 0:
+                    for u in range(2):
+                        state["ya"][u] = psy.tile([P, 2, WHOLE, C], F32, name="yb%d" % u, tag="yb%d" % u)
+                for b in range(4):
+                    mx(state["ya"][b // 2][:, b % 2, e, :], job, b, h_words[e][:], h_bytes[e][:])
+                if e == WHOLE - 1:
+                    for b in range(4):
+                        nc.scalar.copy(
+                            out=ywin[b][:, 0:WHOLE * C],
+                            in_=state["ya"][b // 2][:, b % 2, :, :].rearrange("p e n -> p (e n)"),
+                        )
+            elif kind == "q":
+                b = job["b"]
+                experts = job["experts"]
+                u = 0 if len(experts) == 4 else 1
+                yb = psy.tile([P, len(experts) * C], F32, name="yb%d" % u, tag="yb%d" % u)
+                for i, e in enumerate(experts):
+                    mx(yb[:, i * C:(i + 1) * C], job, i, h_words[e][:], h_bytes[e][:])
+                eng = nc.scalar.copy if u == 0 else nc.vector.tensor_copy
+                eng(out=ywin[b][:, experts[0] * C:(experts[-1] + 1) * C], in_=yb[:])
+            elif kind == "g":
+                combine(job["b"])
+
+        n = len(jobs)
+        for i in range(min(PRE, n)):
+            load(jobs[i])
+        for s in range(n + 3):
+            if s + PRE < n:
+                load(jobs[s + PRE])
+            if 0 <= s - 1 < n:
+                quantise(jobs[s - 1])
+            if 0 <= s - 2 < n:
+                compute(jobs[s - 2])
+            elif s - 2 >= n:
+                run_later()
+            if s < n:
+                interleave(jobs[s])

@@ -1,6 +1,7 @@
 from contextlib import ExitStack
 
 import concourse.mybir as mybir
+from concourse.masks import make_identity
 
 K, T, E, C, H, N = 512, 512, 8, 128, 512, 512
 P = 128
@@ -17,6 +18,16 @@ ADD = mybir.AluOpType.add
 SILU = mybir.ActivationFunctionType.Silu
 
 WHOLE = 2
+PIECES = [[2, 3, 4, 5], [6, 7]]
+QSHARE = [[32, 16], [128, 64], [128, 64], [128, 64]]
+OUT_ENG = ["S", "V"]
+PE_ADD = []
+SPLIT_LAST = 0
+GATE_LATE = 1
+SPLIT_AB = 0
+EARLY_W1 = 0
+COMB_LAG = 0
+WS = {"w1": [80] * 8, "w3": [80] * 8, "w2": [80] * 8}
 RAW_BUFS = 10
 PRE = 9
 S_SHARE = 80
@@ -59,6 +70,10 @@ def tile_routed_moe_kernel(tc, xT, w1, w3, w2, gate, offs, pos1, pos2, out):
         h_bytes = [keep.tile([P, C], U8, name="h_bytes%d" % e, align_bytes=64) for e in range(E)]
         ywin = [keep.tile([P, E * C], F32, name="ywin%d" % b) for b in range(4)]
         gates = [None] * 4
+        ident = None
+        if PE_ADD:
+            ident = keep.tile([P, P], F32, name="ident")
+            make_identity(nc, ident[:])
 
         jobs = [{"kind": "x", "width": 512}]
         for e in range(E):
@@ -66,12 +81,18 @@ def tile_routed_moe_kernel(tc, xT, w1, w3, w2, gate, offs, pos1, pos2, out):
             jobs.append({"kind": "w3", "e": e, "width": 512})
             if 1 <= e <= WHOLE:
                 jobs.append({"kind": "w2", "e": e - 1, "width": 512})
+        if EARLY_W1:
+            late = jobs.pop(len(jobs) - 2)
+            jobs.insert(len(jobs) - 2, late)
         for b in range(4):
-            jobs.append({"kind": "q", "b": b, "experts": [2, 3, 4, 5], "width": 512, "share": 32 if b == 0 else S_SHARE_QA})
-            jobs.append({"kind": "q", "b": b, "experts": [6, 7], "width": 256, "share": 16 if b == 0 else S_SHARE_QB})
+            for u, ex in enumerate(PIECES):
+                jobs.append({"kind": "q", "b": b, "u": u, "experts": ex, "width": len(ex) * P, "share": QSHARE[b][u]})
+            if b >= GATE_LATE:
+                jobs.append({"kind": "g", "b": b - GATE_LATE})
+        for b in range(4 - GATE_LATE, 4):
             jobs.append({"kind": "g", "b": b})
 
-        state = {"ya": [None, None], "w1": {}, "later": []}
+        state = {"ya": [None, None], "w1": {}, "later": [], "sil": {}, "comb": []}
 
         def load(job):
             kind = job["kind"]
@@ -101,7 +122,7 @@ def tile_routed_moe_kernel(tc, xT, w1, w3, w2, gate, offs, pos1, pos2, out):
                 return
             raw = job["raw"]
             groups = job["width"] // 4
-            share = job.get("share", S_SHARE_X if kind == "x" else S_SHARE)
+            share = job["share"] if kind == "q" else (S_SHARE_X if kind == "x" else WS[kind][job["e"]])
             if kind in ("w1", "w3"):
                 grp = grpp.tile([P, 4, 128, 4], BF16, name="grp", tag="grp", align_bytes=64)
                 job["flat"] = grp[:].rearrange("p t m j -> p (t m j)")
@@ -155,20 +176,36 @@ def tile_routed_moe_kernel(tc, xT, w1, w3, w2, gate, offs, pos1, pos2, out):
             )
 
         def combine(b):
+            halves = 2 if (SPLIT_LAST and b == 3) else 1
+            w = T // halves
             parts = []
-            for r in range(2):
-                part = work.tile([P, T], F32, name="part%d" % r, tag="part%d" % r)
-                nc.vector.tensor_tensor(out=part[:], in0=ywin[b][:].indirect(pos_t[r][:]), in1=gates[b][:, r, :], op=MULT)
-                parts.append(part)
-            res = work.tile([P, T], F32, name="res", tag="res")
-            nc.vector.tensor_tensor(out=res[:], in0=parts[0][:], in1=parts[1][:], op=ADD)
-            nc.sync.dma_start(out=out[b * P:(b + 1) * P, :], in_=res[:])
+            for hf in range(halves):
+                for r in range(2):
+                    part = work.tile([P, w], F32, name="part%d" % r, tag="part%d%d" % (r, hf))
+                    nc.vector.tensor_tensor(out=part[:], in0=ywin[b][:].indirect(pos_t[r][:] if halves == 1 else pos_t[r][:, hf * w // 16:(hf + 1) * w // 16]), in1=gates[b][:, r, hf * w:(hf + 1) * w], op=MULT)
+                    parts.append(part)
+            for hf in range(halves):
+                res = work.tile([P, w], F32, name="res", tag="res%d" % hf)
+                if b in PE_ADD:
+                    ps = psab.tile([P, w], F32, name="pa", tag="pa")
+                    nc.tensor.matmul(out=ps[:], lhsT=ident[:], rhs=parts[2 * hf][:], start=True, stop=False)
+                    nc.tensor.matmul(out=ps[:], lhsT=ident[:], rhs=parts[2 * hf + 1][:], start=False, stop=True)
+                    nc.scalar.copy(out=res[:], in_=ps[:])
+                else:
+                    nc.vector.tensor_tensor(out=res[:], in0=parts[2 * hf][:], in1=parts[2 * hf + 1][:], op=ADD)
+                nc.sync.dma_start(out=out[b * P:(b + 1) * P, hf * w:(hf + 1) * w], in_=res[:])
 
         def run_later():
             later = state["later"]
             state["later"] = []
             for fn in later:
                 fn()
+
+        def due_combines():
+            for item in state["comb"]:
+                item[0] -= 1
+            while state["comb"] and state["comb"][0][0] <= 0:
+                combine(state["comb"].pop(0)[1])
 
         def compute(job):
             kind = job["kind"]
@@ -178,56 +215,80 @@ def tile_routed_moe_kernel(tc, xT, w1, w3, w2, gate, offs, pos1, pos2, out):
             elif kind == "w1":
                 e = job["e"]
                 state["w1"][e] = job
+                if SPLIT_AB:
+                    xw = g_words[e // 2][:, (e % 2) * C:(e % 2 + 1) * C]
+                    xs = g_bytes[e // 2][:, (e % 2) * C:(e % 2 + 1) * C]
+                    pa = psab.tile([P, 4, C], F32, name="pa", tag="pa")
+                    for t in range(4):
+                        mx(pa[:, t, :], job, t, xw, xs)
+                    sil = work.tile([P, C, 4], F32, name="sil", tag="sil")
+                    nc.scalar.activation(out=sil[:], in_=pa[:].rearrange("p t n -> p n t"), func=SILU)
+                    state["sil"][e] = sil
                 if e % 2 == 1 and e < E - 1:
                     gather_tokens((e + 1) // 2)
             elif kind == "w3":
                 e = job["e"]
                 xw = g_words[e // 2][:, (e % 2) * C:(e % 2 + 1) * C]
                 xs = g_bytes[e // 2][:, (e % 2) * C:(e % 2 + 1) * C]
-                pa = psab.tile([P, 4, C], F32, name="pa", tag="pa")
                 pb = psab.tile([P, 4, C], F32, name="pb", tag="pb")
-                for t in range(4):
-                    mx(pa[:, t, :], state["w1"][e], t, xw, xs)
+                if not SPLIT_AB:
+                    pa = psab.tile([P, 4, C], F32, name="pa", tag="pa")
+                    for t in range(4):
+                        mx(pa[:, t, :], state["w1"][e], t, xw, xs)
                 for t in range(4):
                     mx(pb[:, t, :], job, t, xw, xs)
-                sil = work.tile([P, C, 4], F32, name="sil", tag="sil")
-                nc.scalar.activation(out=sil[:], in_=pa[:].rearrange("p t n -> p n t"), func=SILU)
+                if SPLIT_AB:
+                    sil = state["sil"][e]
+                else:
+                    sil = work.tile([P, C, 4], F32, name="sil", tag="sil")
+                    nc.scalar.activation(out=sil[:], in_=pa[:].rearrange("p t n -> p n t"), func=SILU)
                 hg = work.tile([P, C, 4], BF16, name="hg", tag="hg", align_bytes=64)
                 nc.vector.tensor_tensor(out=hg[:], in0=pb[:].rearrange("p t n -> p n t"), in1=sil[:], op=MULT)
                 state["later"].append(lambda: quantise_h(e, hg))
             elif kind == "w2":
                 e = job["e"]
                 if e == 0:
-                    for u in range(2):
-                        state["ya"][u] = psy.tile([P, 2, WHOLE, C], F32, name="yb%d" % u, tag="yb%d" % u)
+                    state["ya"] = []
+                    for b in range(4):
+                        if WHOLE > 2:
+                            bank = psy.tile([P, WHOLE, C], F32, name="yb%d" % (b % 2), tag="yb%d" % (b % 2))
+                            state["ya"].append((bank, -1))
+                        else:
+                            if b % 2 == 0:
+                                bank = psy.tile([P, 2, WHOLE, C], F32, name="yb%d" % (b // 2), tag="yb%d" % (b // 2))
+                            state["ya"].append((bank, b % 2))
                 for b in range(4):
-                    mx(state["ya"][b // 2][:, b % 2, e, :], job, b, h_words[e][:], h_bytes[e][:])
+                    bank, half = state["ya"][b]
+                    mx(bank[:, e, :] if half < 0 else bank[:, half, e, :], job, b, h_words[e][:], h_bytes[e][:])
                 if e == WHOLE - 1:
                     for b in range(4):
-                        nc.scalar.copy(
-                            out=ywin[b][:, 0:WHOLE * C],
-                            in_=state["ya"][b // 2][:, b % 2, :, :].rearrange("p e n -> p (e n)"),
-                        )
+                        bank, half = state["ya"][b]
+                        src = bank[:, :, :] if half < 0 else bank[:, half, :, :]
+                        nc.scalar.copy(out=ywin[b][:, 0:WHOLE * C], in_=src.rearrange("p e n -> p (e n)"))
             elif kind == "q":
                 b = job["b"]
                 experts = job["experts"]
-                u = 0 if len(experts) == 4 else 1
+                u = job["u"]
                 yb = psy.tile([P, len(experts) * C], F32, name="yb%d" % u, tag="yb%d" % u)
                 for i, e in enumerate(experts):
                     mx(yb[:, i * C:(i + 1) * C], job, i, h_words[e][:], h_bytes[e][:])
-                eng = nc.scalar.copy if u == 0 else nc.vector.tensor_copy
+                eng = nc.scalar.copy if OUT_ENG[u] == "S" else nc.vector.tensor_copy
                 eng(out=ywin[b][:, experts[0] * C:(experts[-1] + 1) * C], in_=yb[:])
             elif kind == "g":
-                combine(job["b"])
+                if COMB_LAG:
+                    state["comb"].append([COMB_LAG, job["b"]])
+                else:
+                    combine(job["b"])
 
         n = len(jobs)
         for i in range(min(PRE, n)):
             load(jobs[i])
-        for s in range(n + 3):
+        for s in range(n + 3 + COMB_LAG):
             if s + PRE < n:
                 load(jobs[s + PRE])
             if 0 <= s - 1 < n:
                 quantise(jobs[s - 1])
+            due_combines()
             if 0 <= s - 2 < n:
                 compute(jobs[s - 2])
             elif s - 2 >= n:

@@ -24,6 +24,8 @@ OUT_ENG = ["S", "V"]
 PE_ADD = []
 SPLIT_LAST = 0
 GATE_LATE = 1
+WHOLE_LATE = 0
+OUT_V_BLOCKS = [0]
 SPLIT_AB = 0
 EARLY_W1 = 0
 COMB_LAG = 0
@@ -79,8 +81,11 @@ def tile_routed_moe_kernel(tc, xT, w1, w3, w2, gate, offs, pos1, pos2, out):
         for e in range(E):
             jobs.append({"kind": "w1", "e": e, "width": 512})
             jobs.append({"kind": "w3", "e": e, "width": 512})
-            if 1 <= e <= WHOLE:
+            if 1 <= e <= WHOLE and not WHOLE_LATE:
                 jobs.append({"kind": "w2", "e": e - 1, "width": 512})
+        if WHOLE_LATE:
+            for e in range(WHOLE):
+                jobs.append({"kind": "w2", "e": e, "width": 512})
         if EARLY_W1:
             late = jobs.pop(len(jobs) - 2)
             jobs.insert(len(jobs) - 2, late)
@@ -272,7 +277,7 @@ def tile_routed_moe_kernel(tc, xT, w1, w3, w2, gate, offs, pos1, pos2, out):
                 yb = psy.tile([P, len(experts) * C], F32, name="yb%d" % u, tag="yb%d" % u)
                 for i, e in enumerate(experts):
                     mx(yb[:, i * C:(i + 1) * C], job, i, h_words[e][:], h_bytes[e][:])
-                eng = nc.scalar.copy if OUT_ENG[u] == "S" else nc.vector.tensor_copy
+                eng = nc.scalar.copy if (OUT_ENG[u] == "S" and b not in OUT_V_BLOCKS) else nc.vector.tensor_copy
                 eng(out=ywin[b][:, experts[0] * C:(experts[-1] + 1) * C], in_=yb[:])
             elif kind == "g":
                 if COMB_LAG:

@@ -24,7 +24,7 @@ OUT_ENG = ["S", "V"]
 PE_ADD = []
 SPLIT_LAST = 0
 GATE_LATE = 1
-WHOLE_LATE = 0
+WHOLE_LATE = 1
 OUT_V_BLOCKS = [0]
 SPLIT_AB = 0
 EARLY_W1 = 0

from contextlib import ExitStack

import concourse.mybir as mybir
from concourse.masks import make_identity

K, T, E, C, H, N = 512, 512, 8, 128, 512, 512
P = 128
FLOPS = 2 * E * C * (2 * K * H + H * N)

F32 = mybir.dt.float32
BF16 = mybir.dt.bfloat16
U32 = mybir.dt.uint32
U16 = mybir.dt.uint16
U8 = mybir.dt.uint8
FP8X4 = mybir.dt.float8_e4m3fn_x4
MULT = mybir.AluOpType.mult
ADD = mybir.AluOpType.add
SILU = mybir.ActivationFunctionType.Silu

WHOLE = 2
PIECES = [[2, 3, 4, 5], [6, 7]]
QSHARE = [[32, 16], [128, 64], [128, 64], [128, 64]]
OUT_ENG = ["S", "V"]
PE_ADD = []
SPLIT_LAST = 0
GATE_LATE = 1
WHOLE_LATE = 1
OUT_V_BLOCKS = [0]
SPLIT_AB = 0
EARLY_W1 = 0
COMB_LAG = 0
WS = {"w1": [80] * 8, "w3": [80] * 8, "w2": [80] * 8}
RAW_BUFS = 10
PRE = 9
S_SHARE = 80
S_SHARE_X = 44
S_SHARE_QA = 128
S_SHARE_QB = 64


def tile_routed_moe_kernel(tc, xT, w1, w3, w2, gate, offs, pos1, pos2, out):
    nc = tc.nc
    with ExitStack() as ctx:
        lists = ctx.enter_context(tc.tile_pool(name="lists", bufs=1))
        keep = ctx.enter_context(tc.tile_pool(name="keep", bufs=1))
        rawp = ctx.enter_context(tc.tile_pool(name="rawp", bufs=RAW_BUFS))
        grpp = ctx.enter_context(tc.tile_pool(name="grpp", bufs=4))
        codp = ctx.enter_context(tc.tile_pool(name="codp", bufs=4))
        work = ctx.enter_context(tc.tile_pool(name="work", bufs=2))
        psab = ctx.enter_context(tc.psum_pool(name="psab", bufs=2))
        psy = ctx.enter_context(tc.psum_pool(name="psy", bufs=2))

        offs_t = lists.tile([P, E * C // 16], U16, name="offs_t")
        nc.sync.dma_start(offs_t[:], offs)
        pos1_t = lists.tile([P, T // 16], U16, name="pos1_t")
        nc.sync.dma_start(pos1_t[:], pos1)
        pos2_t = lists.tile([P, T // 16], U16, name="pos2_t")
        nc.sync.dma_start(pos2_t[:], pos2)
        pos_t = [pos1_t, pos2_t]

        warm = keep.tile([P, 1], F32, name="warm")
        nc.vector.memset(warm[:], 0.0)
        warm2 = keep.tile([P, 1], F32, name="warm2")
        nc.scalar.activation(out=warm2[:], in_=warm[:], func=SILU)

        x_words = keep.tile([P, T], U32, name="x_words", align_bytes=64)
        x_bytes = keep.tile([P, T], U8, name="x_bytes", align_bytes=64)
        nc.gpsimd.memset(x_bytes[:], 0)
        g_words = [keep.tile([P, 2 * C], U32, name="g_words%d" % s, align_bytes=64) for s in range(4)]
        g_bytes = [keep.tile([P, 2 * C], U8, name="g_bytes%d" % s, align_bytes=64) for s in range(4)]
        h_words = [keep.tile([P, C], U32, name="h_words%d" % e, align_bytes=64) for e in range(E)]
        h_bytes = [keep.tile([P, C], U8, name="h_bytes%d" % e, align_bytes=64) for e in range(E)]
        ywin = [keep.tile([P, E * C], F32, name="ywin%d" % b) for b in range(4)]
        gates = [None] * 4
        ident = None
        if PE_ADD:
            ident = keep.tile([P, P], F32, name="ident")
            make_identity(nc, ident[:])

        jobs = [{"kind": "x", "width": 512}]
        for e in range(E):
            jobs.append({"kind": "w1", "e": e, "width": 512})
            jobs.append({"kind": "w3", "e": e, "width": 512})
            if 1 <= e <= WHOLE and not WHOLE_LATE:
                jobs.append({"kind": "w2", "e": e - 1, "width": 512})
        if WHOLE_LATE:
            for e in range(WHOLE):
                jobs.append({"kind": "w2", "e": e, "width": 512})
        if EARLY_W1:
            late = jobs.pop(len(jobs) - 2)
            jobs.insert(len(jobs) - 2, late)
        for b in range(4):
            for u, ex in enumerate(PIECES):
                jobs.append({"kind": "q", "b": b, "u": u, "experts": ex, "width": len(ex) * P, "share": QSHARE[b][u]})
            if b >= GATE_LATE:
                jobs.append({"kind": "g", "b": b - GATE_LATE})
        for b in range(4 - GATE_LATE, 4):
            jobs.append({"kind": "g", "b": b})

        state = {"ya": [None, None], "w1": {}, "later": [], "sil": {}, "comb": []}

        def load(job):
            kind = job["kind"]
            if kind == "g":
                b = job["b"]
                gates[b] = rawp.tile([P, 2, T], F32, name="raw", tag="raw")
                nc.sync.dma_start(out=gates[b][:], in_=gate[:, b * P:(b + 1) * P, :].rearrange("r p t -> p r t"))
                return
            raw = rawp.tile([P, 4, job["width"]], F32, name="raw", tag="raw")
            job["raw"] = raw
            if kind == "x":
                nc.sync.dma_start(out=raw[:], in_=xT.rearrange("(p j) c -> p j c", j=4))
            elif kind == "q":
                b = job["b"]
                for i, e in enumerate(job["experts"]):
                    nc.sync.dma_start(
                        out=raw[:, :, i * P:(i + 1) * P],
                        in_=w2[e].rearrange("(p j) c -> p j c", j=4)[:, :, b * P:(b + 1) * P],
                    )
            else:
                src = {"w1": w1, "w3": w3, "w2": w2}[kind]
                nc.sync.dma_start(out=raw[:], in_=src[job["e"]].rearrange("(p j) c -> p j c", j=4))

        def interleave(job):
            kind = job["kind"]
            if kind == "g":
                return
            raw = job["raw"]
            groups = job["width"] // 4
            share = job["share"] if kind == "q" else (S_SHARE_X if kind == "x" else WS[kind][job["e"]])
            if kind in ("w1", "w3"):
                grp = grpp.tile([P, 4, 128, 4], BF16, name="grp", tag="grp", align_bytes=64)
                job["flat"] = grp[:].rearrange("p t m j -> p (t m j)")
            else:
                grp = grpp.tile([P, job["width"], 4], BF16, name="grp", tag="grp", align_bytes=64)
                job["flat"] = grp[:].rearrange("p c j -> p (c j)")
            for eng, lo, hi in ((nc.scalar.copy, 0, share), (nc.vector.tensor_copy, share, groups)):
                if lo == hi:
                    continue
                if kind in ("w1", "w3"):
                    dst = grp[:, :, lo:hi, :].rearrange("p t m j -> p m j t")
                    src = raw[:, :, 4 * lo:4 * hi].rearrange("p j (m t) -> p m j t", t=4)
                else:
                    dst = grp[:, 4 * lo:4 * hi, :].rearrange("p (c i) j -> p c j i", i=4)
                    src = raw[:, :, 4 * lo:4 * hi].rearrange("p j (c i) -> p c j i", i=4)
                eng(out=dst, in_=src)

        def quantise(job):
            kind = job["kind"]
            if kind == "g":
                return
            if kind == "x":
                words, scales = x_words, x_bytes
            else:
                words = codp.tile([P, job["width"]], U32, name="words", tag="words", align_bytes=64)
                scales = codp.tile([P, job["width"]], U8, name="scales", tag="scales", align_bytes=64)
            job["words"] = words
            job["scales"] = scales
            nc.vector.quantize_mx(out=words[:].bitcast(FP8X4), scales=scales[:], in_=job["flat"])

        def gather_tokens(s):
            sl = offs_t[:, s * 16:(s + 1) * 16]
            nc.vector.tensor_copy(g_words[s][:], x_words[:].indirect(sl))
            nc.vector.tensor_copy(g_bytes[s][:], x_bytes[:].indirect(sl))

        def mx(out_ap, wjob, col, rhs_w, rhs_s):
            cols = slice(col * P, (col + 1) * P)
            nc.tensor.matmul_mx(
                out=out_ap,
                lhsT=wjob["words"][:, cols].bitcast(FP8X4),
                lhsT_scale=wjob["scales"][:, cols],
                rhs=rhs_w.bitcast(FP8X4),
                rhs_scale=rhs_s,
                start=True,
                stop=True,
            )

        def quantise_h(e, hg):
            nc.vector.quantize_mx(
                out=h_words[e][:].bitcast(FP8X4), scales=h_bytes[e][:], in_=hg[:].rearrange("p n t -> p (n t)")
            )

        def combine(b):
            halves = 2 if (SPLIT_LAST and b == 3) else 1
            w = T // halves
            parts = []
            for hf in range(halves):
                for r in range(2):
                    part = work.tile([P, w], F32, name="part%d" % r, tag="part%d%d" % (r, hf))
                    nc.vector.tensor_tensor(out=part[:], in0=ywin[b][:].indirect(pos_t[r][:] if halves == 1 else pos_t[r][:, hf * w // 16:(hf + 1) * w // 16]), in1=gates[b][:, r, hf * w:(hf + 1) * w], op=MULT)
                    parts.append(part)
            for hf in range(halves):
                res = work.tile([P, w], F32, name="res", tag="res%d" % hf)
                if b in PE_ADD:
                    ps = psab.tile([P, w], F32, name="pa", tag="pa")
                    nc.tensor.matmul(out=ps[:], lhsT=ident[:], rhs=parts[2 * hf][:], start=True, stop=False)
                    nc.tensor.matmul(out=ps[:], lhsT=ident[:], rhs=parts[2 * hf + 1][:], start=False, stop=True)
                    nc.scalar.copy(out=res[:], in_=ps[:])
                else:
                    nc.vector.tensor_tensor(out=res[:], in0=parts[2 * hf][:], in1=parts[2 * hf + 1][:], op=ADD)
                nc.sync.dma_start(out=out[b * P:(b + 1) * P, hf * w:(hf + 1) * w], in_=res[:])

        def run_later():
            later = state["later"]
            state["later"] = []
            for fn in later:
                fn()

        def due_combines():
            for item in state["comb"]:
                item[0] -= 1
            while state["comb"] and state["comb"][0][0] <= 0:
                combine(state["comb"].pop(0)[1])

        def compute(job):
            kind = job["kind"]
            run_later()
            if kind == "x":
                gather_tokens(0)
            elif kind == "w1":
                e = job["e"]
                state["w1"][e] = job
                if SPLIT_AB:
                    xw = g_words[e // 2][:, (e % 2) * C:(e % 2 + 1) * C]
                    xs = g_bytes[e // 2][:, (e % 2) * C:(e % 2 + 1) * C]
                    pa = psab.tile([P, 4, C], F32, name="pa", tag="pa")
                    for t in range(4):
                        mx(pa[:, t, :], job, t, xw, xs)
                    sil = work.tile([P, C, 4], F32, name="sil", tag="sil")
                    nc.scalar.activation(out=sil[:], in_=pa[:].rearrange("p t n -> p n t"), func=SILU)
                    state["sil"][e] = sil
                if e % 2 == 1 and e < E - 1:
                    gather_tokens((e + 1) // 2)
            elif kind == "w3":
                e = job["e"]
                xw = g_words[e // 2][:, (e % 2) * C:(e % 2 + 1) * C]
                xs = g_bytes[e // 2][:, (e % 2) * C:(e % 2 + 1) * C]
                pb = psab.tile([P, 4, C], F32, name="pb", tag="pb")
                if not SPLIT_AB:
                    pa = psab.tile([P, 4, C], F32, name="pa", tag="pa")
                    for t in range(4):
                        mx(pa[:, t, :], state["w1"][e], t, xw, xs)
                for t in range(4):
                    mx(pb[:, t, :], job, t, xw, xs)
                if SPLIT_AB:
                    sil = state["sil"][e]
                else:
                    sil = work.tile([P, C, 4], F32, name="sil", tag="sil")
                    nc.scalar.activation(out=sil[:], in_=pa[:].rearrange("p t n -> p n t"), func=SILU)
                hg = work.tile([P, C, 4], BF16, name="hg", tag="hg", align_bytes=64)
                nc.vector.tensor_tensor(out=hg[:], in0=pb[:].rearrange("p t n -> p n t"), in1=sil[:], op=MULT)
                state["later"].append(lambda: quantise_h(e, hg))
            elif kind == "w2":
                e = job["e"]
                if e == 0:
                    state["ya"] = []
                    for b in range(4):
                        if WHOLE > 2:
                            bank = psy.tile([P, WHOLE, C], F32, name="yb%d" % (b % 2), tag="yb%d" % (b % 2))
                            state["ya"].append((bank, -1))
                        else:
                            if b % 2 == 0:
                                bank = psy.tile([P, 2, WHOLE, C], F32, name="yb%d" % (b // 2), tag="yb%d" % (b // 2))
                            state["ya"].append((bank, b % 2))
                for b in range(4):
                    bank, half = state["ya"][b]
                    mx(bank[:, e, :] if half < 0 else bank[:, half, e, :], job, b, h_words[e][:], h_bytes[e][:])
                if e == WHOLE - 1:
                    for b in range(4):
                        bank, half = state["ya"][b]
                        src = bank[:, :, :] if half < 0 else bank[:, half, :, :]
                        nc.scalar.copy(out=ywin[b][:, 0:WHOLE * C], in_=src.rearrange("p e n -> p (e n)"))
            elif kind == "q":
                b = job["b"]
                experts = job["experts"]
                u = job["u"]
                yb = psy.tile([P, len(experts) * C], F32, name="yb%d" % u, tag="yb%d" % u)
                for i, e in enumerate(experts):
                    mx(yb[:, i * C:(i + 1) * C], job, i, h_words[e][:], h_bytes[e][:])
                eng = nc.scalar.copy if (OUT_ENG[u] == "S" and b not in OUT_V_BLOCKS) else nc.vector.tensor_copy
                eng(out=ywin[b][:, experts[0] * C:(experts[-1] + 1) * C], in_=yb[:])
            elif kind == "g":
                if COMB_LAG:
                    state["comb"].append([COMB_LAG, job["b"]])
                else:
                    combine(job["b"])

        n = len(jobs)
        for i in range(min(PRE, n)):
            load(jobs[i])
        for s in range(n + 3 + COMB_LAG):
            if s + PRE < n:
                load(jobs[s + PRE])
            if 0 <= s - 1 < n:
                quantise(jobs[s - 1])
            due_combines()
            if 0 <= s - 2 < n:
                compute(jobs[s - 2])
            elif s - 2 >= n:
                run_later()
            if s < n:
                interleave(jobs[s])
